import numpy as np
import ml_dtypes


def mxq(x, axis, fmt="e4m3"):
    dtype, down = {"e4m3": (ml_dtypes.float8_e4m3fn, 7), "e5m2": (ml_dtypes.float8_e5m2, 14)}[fmt]
    v = np.moveaxis(np.asarray(x, np.float32).astype(ml_dtypes.bfloat16).astype(np.float64), axis, -1)
    blocks = v.reshape(v.shape[:-1] + (-1, 32))
    amax = np.abs(blocks).max(-1, keepdims=True)
    byte = np.maximum(np.where(amax > 0, np.frexp(amax)[1] - 1 + 127, 0) - down, 1)
    scale = np.exp2(byte - 127.0)
    codes = (blocks / scale).astype(np.float32).astype(dtype).astype(np.float64)
    return np.moveaxis((codes * scale).reshape(v.shape), -1, axis)


WIDE = False


def mx_kscale(k):
    if not WIDE:
        return np.ones(k)
    levels = np.array([10, -10, 5, -5, 0])
    if k % 512:
        return np.exp2(np.random.permutation(np.resize(levels, k // 32))).repeat(32)
    a = np.empty((k // 512, 16))
    for p in range(k // 512):
        a[p, :8] = np.random.permutation(np.resize(levels, 8))
        for g in range(8):
            far = levels[np.abs(levels - a[p, g]) >= 10]
            a[p, g + 8] = far[np.random.randint(len(far))]
    return np.exp2(a.ravel()).repeat(32)


def f64(x):
    return np.asarray(x).astype(np.float64)


def striped(idx):
    return np.tile(idx.reshape(-1, 16).T, (8, 1)).astype(np.uint16)


def unstriped(offs):
    return offs[:16].T.reshape(-1).astype(np.int64)


E2M1 = np.array([0.0, 0.5, 1.0, 1.5, 2.0, 3.0, 4.0, 6.0, -0.0, -0.5, -1.0, -1.5, -2.0, -3.0, -4.0, -6.0])


def pack_weight(w, fmt):
    k, n = w.shape
    w = f64(np.asarray(w, np.float32).astype(ml_dtypes.bfloat16)).reshape(k // 32, 32, n)
    amax = np.abs(w).max(1)
    if fmt == "e4m3":
        byte = np.frexp(amax)[1] - 1 + 127 - 7
    else:
        mant, ex = np.frexp(amax / 6.0)
        byte = np.where(mant > 0.5, ex, ex - 1) + 127
    byte = np.clip(np.where(amax > 0, byte, 1), 1, 254)
    scaled = (w * np.exp2(127.0 - byte)[:, None, :]).reshape(k, n).astype(np.float32)
    by_word = np.ascontiguousarray(scaled.reshape(k // 512, 128, 4, n).transpose(0, 1, 3, 2))
    if fmt == "e4m3":
        words = by_word.astype(ml_dtypes.float8_e4m3fn).view(np.uint8)
    else:
        c = by_word.astype(ml_dtypes.float4_e2m1fn).view(np.uint8) & 0xF
        words = (c[..., 0::2] | (c[..., 1::2] << 4)).reshape(k // 512, 128, 2 * n)
    return np.ascontiguousarray(words), np.ascontiguousarray(byte.astype(np.uint8).reshape(k // 512, 16, n))


def unpack_weight(words, scales, fmt):
    g, _, n = scales.shape
    words = np.ascontiguousarray(words).reshape(g, 128, n, -1)
    if fmt == "e4m3":
        vals = words.view(ml_dtypes.float8_e4m3fn).astype(np.float64)
    else:
        nib = np.empty((g, 128, n, 4), np.uint8)
        nib[..., 0::2] = words & 0xF
        nib[..., 1::2] = words >> 4
        vals = E2M1[nib]
    vals = vals * np.repeat(np.exp2(scales.astype(np.float64) - 127.0), 8, axis=1)[..., None]
    return vals.transpose(0, 1, 3, 2).reshape(g * 512, n)


def gelu(v):
    return 0.5 * v * (1.0 + np.tanh(np.sqrt(2.0 / np.pi) * (v + 0.044715 * v**3)))


K, T, S, H, T3, S2 = 1536, 2048, 512, 1024, 2048, 512

def setup_inputs():
    n = np.random.standard_normal
    s = mx_kscale(K)[:, None]
    u = mx_kscale(H)[:, None]
    tab_words, tab_scales = pack_weight(n((K, T)) * s, "e4m3")
    tab2_words, tab2_scales = pack_weight(1.5 * n((H, T3)) / np.sqrt(H) / u, "e4m3")
    tab3_words, tab3_scales = pack_weight(2.0 * n((H, T3)) / np.sqrt(H) / u, "e4m3")
    return {
        "tab_words": tab_words,
        "tab_scales": tab_scales,
        "offs": striped(np.random.permutation(T)[:S]),
        "tab2_words": tab2_words,
        "tab2_scales": tab2_scales,
        "offs2": striped(np.random.permutation(T3)[:S2]),
        "tab3_words": tab3_words,
        "tab3_scales": tab3_scales,
        "offs3": striped(np.random.permutation(T3)[:S2]),
        "w1": (n((K, H)) / np.sqrt(K) / s).astype(np.float32),
        "res": (0.9 * n((H, S))).astype(np.float32),
        "gain": (np.exp(0.3 * n(H)) * u[:, 0]).astype(np.float32),
        "low": (0.6 * n(S2)).astype(np.float32),
    }

def reference(tab_words, tab_scales, offs, tab2_words, tab2_scales, offs2,
              tab3_words, tab3_scales, offs3, w1, res, gain, low):
    v = unpack_weight(tab_words, tab_scales, "e4m3")[:, unstriped(offs)]
    v2 = unpack_weight(tab2_words, tab2_scales, "e4m3")[:, unstriped(offs2)]
    v3 = unpack_weight(tab3_words, tab3_scales, "e4m3")[:, unstriped(offs3)]
    w1q = mxq(f64(w1), 0, "e4m3")
    h = f64(gain)[:, None] * np.tanh((w1q.T @ v) + f64(res))
    hq = mxq(h, 0, "e4m3")
    e2 = v2.T @ hq
    e3 = v3.T @ hq
    return np.maximum(e2, f64(low)[:, None]) * np.tanh(e3)

@@ -1,0 +1,222 @@
+from contextlib import ExitStack
+
+import concourse.mybir as mybir
+
+K, T, S, H, T3, S2 = 1536, 2048, 512, 1024, 2048, 512
+FLOPS = 2 * K * H * S + 2 * 2 * H * S2 * S
+
+F32 = mybir.dt.float32
+BF16 = mybir.dt.bfloat16
+I32 = mybir.dt.int32
+U32 = mybir.dt.uint32
+U16 = mybir.dt.uint16
+U8 = mybir.dt.uint8
+FP8X4 = mybir.dt.float8_e4m3fn_x4
+ALU = mybir.AluOpType
+ACT = mybir.ActivationFunctionType
+
+P = 128
+PACK = 4
+K_PASS = P * PACK
+KP = K // K_PASS
+HP = H // K_PASS
+HALF = S // 2
+
+
+def tile_list_cohousing_household_scores_kernel(
+    tc, tab_words, tab_scales, offs, tab2_words, tab2_scales, offs2,
+    tab3_words, tab3_scales, offs3, w1, res, gain, low, out,
+):
+    nc = tc.nc
+    with ExitStack() as ctx:
+        lists = ctx.enter_context(tc.tile_pool(name="lists", bufs=1))
+        keep = ctx.enter_context(tc.tile_pool(name="keep", bufs=1))
+        ring = ctx.enter_context(tc.tile_pool(name="ring", bufs=2))
+        psum = ctx.enter_context(tc.psum_pool(name="psum", bufs=1))
+
+        def load_list(src, name):
+            t = lists.tile([P, S // 16], U16, name=name)
+            nc.sync.dma_start(t[:], src)
+            return t
+
+        def load_words(words, a, name):
+            t = keep.tile([P, T], U32, name=name, align_bytes=64)
+            nc.sync.dma_start(out=t[:].bitcast(I32), in_=words[a].rearrange("p n t -> p (n t)").bitcast(I32))
+            return t
+
+        def load_scales(scales, passes, row0, name, queue):
+            t = keep.tile([P, T], U8, name=name, align_bytes=64)
+            nc.vector.memset(t[:].bitcast(I32), 0)
+            for q in range(4):
+                queue.dma_start(
+                    out=t[32 * q + row0 : 32 * q + row0 + 4 * passes, :].bitcast(I32),
+                    in_=scales[:, 4 * q : 4 * q + 4, :].bitcast(I32),
+                )
+            return t
+
+        def gather(window, lst, e0, n, dtype, name):
+            g = keep.tile([P, n], dtype, name=name, align_bytes=64)
+            nc.vector.tensor_copy(out=g[:], in_=window[:].indirect(lst[:, e0 // 16 : (e0 + n) // 16]))
+            return g
+
+        def load_w(b, a):
+            t = keep.tile([P, PACK, K_PASS], F32, name=f"w_raw{b}{a}")
+            rows = w1[a * K_PASS : (a + 1) * K_PASS, b * K_PASS : (b + 1) * K_PASS]
+            nc.sync.dma_start(out=t[:], in_=rows.rearrange("(p j) c -> p j c", j=PACK))
+            return t
+
+        def load_res(b):
+            t = keep.tile([P, PACK, S], F32, name=f"res{b}")
+            nc.sync.dma_start(out=t[:], in_=res[b * K_PASS : (b + 1) * K_PASS, :].rearrange("(p t) j -> p t j", t=PACK))
+            return t
+
+        w_ops = {}
+
+        def cast_w(raw, b, a, t0, nt, copy):
+            g = keep.tile([P, nt * K_PASS], BF16, name=f"w_bf{b}{a}{t0}", tag=f"w_bf{a}_{t0}", align_bytes=64)
+            copy(
+                out=g[:].rearrange("p (t m j) -> p m j t", t=nt, j=PACK),
+                in_=raw[:].rearrange("p j (m t) -> p m j t", t=PACK)[:, :, :, t0 : t0 + nt],
+            )
+            return g
+
+        def quant_w(g, b, a, t0, nt):
+            codes = keep.tile([P, nt * P], U32, name=f"w_codes{b}{a}{t0}", align_bytes=64)
+            scales = keep.tile([P, nt * P], U8, name=f"w_scales{b}{a}{t0}", align_bytes=64)
+            nc.vector.quantize_mx(out=codes[:].bitcast(FP8X4), scales=scales[:], in_=g[:])
+            for t in range(nt):
+                w_ops[(b, a, t0 + t)] = (codes[:, t * P : (t + 1) * P], scales[:, t * P : (t + 1) * P])
+
+        sc1 = load_scales(tab_scales, KP, 0, "sc1", nc.gpsimd)
+        sc3 = load_scales(tab3_scales, HP, 0, "sc3", nc.gpsimd)
+        sc2 = load_scales(tab2_scales, HP, 8, "sc2", nc.gpsimd)
+        w_raw = {}
+        words1 = []
+        w_raw[(0, 0)] = load_w(0, 0)
+        list1 = load_list(offs, "list1")
+        words1.append(load_words(tab_words, 0, "words1_0"))
+        w_raw[(0, 1)] = load_w(0, 1)
+        list3 = load_list(offs3, "list3")
+        list2 = load_list(offs2, "list2")
+        gain_sb = keep.tile([P, HP, PACK], F32, name="gain_sb")
+        nc.scalar.dma_start(out=gain_sb[:], in_=gain.rearrange("(b p t) -> p b t", b=HP, t=PACK))
+        low_sb = keep.tile([P, S2 // P], F32, name="low_sb")
+        with nc.allow_non_contiguous_dma(reason="one level a partition"):
+            nc.scalar.dma_start(out=low_sb[:], in_=low.rearrange("(c p) -> p c", p=P))
+        words1.append(load_words(tab_words, 1, "words1_1"))
+        w_raw[(0, 2)] = load_w(0, 2)
+        words1.append(load_words(tab_words, 2, "words1_2"))
+        res_sb = [load_res(0)]
+        for a in range(KP):
+            w_raw[(1, a)] = load_w(1, a)
+        res_sb.append(load_res(1))
+        words3 = [load_words(tab3_words, b, f"words3_{b}") for b in range(HP)]
+        words2 = [load_words(tab2_words, b, f"words2_{b}") for b in range(HP)]
+
+        banks = {}
+
+        def stage1_pass(b, a, v_words, v_scales):
+            for t in range(PACK):
+                if a == 0:
+                    banks[(b, t)] = psum.tile([P, S], F32, name=f"h_acc{b}{t}", tag=f"bank{b}{t}")
+                codes, scales = w_ops[(b, a, t)]
+                nc.tensor.matmul_mx(
+                    out=banks[(b, t)][:], lhsT=codes.bitcast(FP8X4), lhsT_scale=scales,
+                    rhs=v_words[a][:].bitcast(FP8X4), rhs_scale=v_scales[4 * a : P, :],
+                    start=(a == 0), stop=(a == KP - 1),
+                )
+
+        h_codes = [keep.tile([P, S], U32, name=f"h_codes{b}", align_bytes=64) for b in range(HP)]
+        h_scales = [keep.tile([P, S], U8, name=f"h_scales{b}", align_bytes=64) for b in range(HP)]
+
+        def h_add_tanh(b, hf):
+            cols = slice(hf * HALF, (hf + 1) * HALF)
+            x = ring.tile([P, PACK, HALF], F32, name="x")
+            for t in range(PACK):
+                nc.vector.tensor_tensor(out=x[:, t, :], in0=banks[(b, t)][:, cols], in1=res_sb[b][:, t, cols], op=ALU.add)
+            th = ring.tile([P, HALF, PACK], F32, name="th")
+            nc.scalar.activation(
+                out=th[:].rearrange("p (c i) t -> p c t i", i=4),
+                in_=x[:].rearrange("p t (c i) -> p c t i", i=4),
+                func=ACT.Tanh,
+            )
+            return th
+
+        def h_gain(b, th):
+            hb = ring.tile([P, HALF, PACK], BF16, name="hb", align_bytes=64)
+            nc.vector.tensor_tensor(
+                out=hb[:], in0=th[:], in1=gain_sb[:, b : b + 1, :].broadcast_to([P, HALF, PACK]), op=ALU.mult
+            )
+            return hb
+
+        def h_quant(b, hf, hb):
+            cols = slice(hf * HALF, (hf + 1) * HALF)
+            nc.vector.quantize_mx(
+                out=h_codes[b][:, cols].bitcast(FP8X4), scales=h_scales[b][:, cols],
+                in_=hb[:].rearrange("p c t -> p (c t)"),
+            )
+
+        def stage2_pass(acc, b, words, scales, row0, c, c0):
+            nc.tensor.matmul_mx(
+                out=acc[:], lhsT=words[:, c0 : c0 + P].bitcast(FP8X4),
+                lhsT_scale=scales[row0 + 4 * b : P, c * P : (c + 1) * P],
+                rhs=h_codes[b][:].bitcast(FP8X4), rhs_scale=h_scales[b][:],
+                start=(b == 0), stop=(b == HP - 1),
+            )
+
+        v_scales = gather(sc1, list1, 0, S, U8, "v_scales")
+        v_words = []
+        for a in range(KP):
+            if a == KP - 1:
+                v3_scales = gather(sc3, list3, 0, S2, U8, "v3_scales")
+                v2_scales = gather(sc2, list2, 0, S2, U8, "v2_scales")
+            g = cast_w(w_raw[(0, a)], 0, a, 0, PACK, nc.scalar.copy)
+            v_words.append(gather(words1[a], list1, 0, S, U32, f"v_words{a}"))
+            quant_w(g, 0, a, 0, PACK)
+            stage1_pass(0, a, v_words, v_scales)
+        ths = [h_add_tanh(0, hf) for hf in range(2)]
+        g10 = cast_w(w_raw[(1, 0)], 1, 0, 0, PACK, nc.scalar.copy)
+        hbs = [h_gain(0, th) for th in ths]
+        g11 = cast_w(w_raw[(1, 1)], 1, 1, 0, PACK, nc.vector.tensor_copy)
+        for hf in range(2):
+            h_quant(0, hf, hbs[hf])
+        quant_w(g11, 1, 1, 0, PACK)
+        quant_w(g10, 1, 0, 0, PACK)
+        stage1_pass(1, 0, v_words, v_scales)
+        stage1_pass(1, 1, v_words, v_scales)
+        g12a = cast_w(w_raw[(1, 2)], 1, 2, 0, 2, nc.scalar.copy)
+        g12b = cast_w(w_raw[(1, 2)], 1, 2, 2, 2, nc.vector.tensor_copy)
+        quant_w(g12a, 1, 2, 0, 2)
+        quant_w(g12b, 1, 2, 2, 2)
+        stage1_pass(1, 2, v_words, v_scales)
+        ths = [h_add_tanh(1, hf) for hf in range(2)]
+
+        MT = S2 // P
+        e3 = [psum.tile([P, S], F32, name=f"e3_{c}", tag=f"bank0{c}") for c in range(MT)]
+        e2 = [psum.tile([P, S], F32, name=f"e2_{c}", tag=f"bank1{c}") for c in range(MT)]
+        g3 = gather(words3[0], list3, 0, S2, U32, "v3_words0")
+        for c in range(MT):
+            stage2_pass(e3[c], 0, g3, v3_scales, 0, c, c * P)
+        hbs = [h_gain(1, th) for th in ths]
+        g3 = gather(words3[1], list3, 0, S2, U32, "v3_words1")
+        for hf in range(2):
+            h_quant(1, hf, hbs[hf])
+        for c in range(MT):
+            stage2_pass(e3[c], 1, g3, v3_scales, 0, c, c * P)
+        th3 = []
+        for c in range(MT):
+            t3 = keep.tile([P, S], F32, name=f"th3_{c}")
+            nc.scalar.activation(out=t3[:], in_=e3[c][:], func=ACT.Tanh)
+            th3.append(t3)
+        g2 = gather(words2[0], list2, 0, S2, U32, "v2_words0")
+        for c in range(MT):
+            stage2_pass(e2[c], 0, g2, v2_scales, 8, c, c * P)
+        for c in range(MT):
+            g2c = gather(words2[1], list2, c * P, P, U32, f"v2_words1_{c}")
+            stage2_pass(e2[c], 1, g2c, v2_scales, 8, c, 0)
+        for c in range(MT):
+            o = keep.tile([P, S], F32, name=f"o{c}")
+            nc.vector.scalar_tensor_tensor(
+                out=o[:], in0=e2[c][:], scalar=low_sb[:, c : c + 1], in1=th3[c][:], op0=ALU.max, op1=ALU.mult
+            )
+            nc.sync.dma_start(out=out[c * P : (c + 1) * P, :], in_=o[:])

@@ -21,6 +21,7 @@ K_PASS = P * PACK
 KP = K // K_PASS
 HP = H // K_PASS
 HALF = S // 2
+MT = S2 // P
 
 
 def tile_list_cohousing_household_scores_kernel(
@@ -31,8 +32,10 @@ def tile_list_cohousing_household_scores_kernel(
     with ExitStack() as ctx:
         lists = ctx.enter_context(tc.tile_pool(name="lists", bufs=1))
         keep = ctx.enter_context(tc.tile_pool(name="keep", bufs=1))
-        ring = ctx.enter_context(tc.tile_pool(name="ring", bufs=2))
         psum = ctx.enter_context(tc.psum_pool(name="psum", bufs=1))
+
+        def sb(shape, dtype, name, slot=None):
+            return keep.tile(shape, dtype, name=name, tag=slot or name, align_bytes=64)
 
         def load_list(src, name):
             t = lists.tile([P, S // 16], U16, name=name)
@@ -40,83 +43,57 @@ def tile_list_cohousing_household_scores_kernel(
             return t
 
         def load_words(words, a, name):
-            t = keep.tile([P, T], U32, name=name, align_bytes=64)
+            t = sb([P, T], U32, name)
             nc.sync.dma_start(out=t[:].bitcast(I32), in_=words[a].rearrange("p n t -> p (n t)").bitcast(I32))
             return t
 
-        def load_scales(scales, passes, row0, name, queue):
-            t = keep.tile([P, T], U8, name=name, align_bytes=64)
+        def load_scales(scales, passes, row0, name):
+            t = sb([P, T], U8, name)
             nc.vector.memset(t[:].bitcast(I32), 0)
             for q in range(4):
-                queue.dma_start(
+                nc.gpsimd.dma_start(
                     out=t[32 * q + row0 : 32 * q + row0 + 4 * passes, :].bitcast(I32),
                     in_=scales[:, 4 * q : 4 * q + 4, :].bitcast(I32),
                 )
             return t
 
-        def gather(window, lst, e0, n, dtype, name):
-            g = keep.tile([P, n], dtype, name=name, align_bytes=64)
-            nc.vector.tensor_copy(out=g[:], in_=window[:].indirect(lst[:, e0 // 16 : (e0 + n) // 16]))
+        def gather(window, lst, dtype, name, slot=None):
+            g = sb([P, S], dtype, name, slot)
+            nc.vector.tensor_copy(out=g[:], in_=window[:].indirect(lst[:]))
             return g
 
         def load_w(b, a):
-            t = keep.tile([P, PACK, K_PASS], F32, name=f"w_raw{b}{a}")
+            t = sb([P, PACK, K_PASS], F32, f"w_raw{b}{a}")
             rows = w1[a * K_PASS : (a + 1) * K_PASS, b * K_PASS : (b + 1) * K_PASS]
             nc.sync.dma_start(out=t[:], in_=rows.rearrange("(p j) c -> p j c", j=PACK))
             return t
 
         def load_res(b):
-            t = keep.tile([P, PACK, S], F32, name=f"res{b}")
+            t = sb([P, PACK, S], F32, f"res{b}")
             nc.sync.dma_start(out=t[:], in_=res[b * K_PASS : (b + 1) * K_PASS, :].rearrange("(p t) j -> p t j", t=PACK))
             return t
 
         w_ops = {}
 
-        def cast_w(raw, b, a, t0, nt, copy):
-            g = keep.tile([P, nt * K_PASS], BF16, name=f"w_bf{b}{a}{t0}", tag=f"w_bf{a}_{t0}", align_bytes=64)
+        def cast_w(b, a, t0, nt, copy, slot=None):
+            g = sb([P, nt * K_PASS], BF16, f"w_bf{b}{a}{t0}", slot)
             copy(
                 out=g[:].rearrange("p (t m j) -> p m j t", t=nt, j=PACK),
-                in_=raw[:].rearrange("p j (m t) -> p m j t", t=PACK)[:, :, :, t0 : t0 + nt],
+                in_=w_raw[(b, a)][:].rearrange("p j (m t) -> p m j t", t=PACK)[:, :, :, t0 : t0 + nt],
             )
             return g
 
-        def quant_w(g, b, a, t0, nt):
-            codes = keep.tile([P, nt * P], U32, name=f"w_codes{b}{a}{t0}", align_bytes=64)
-            scales = keep.tile([P, nt * P], U8, name=f"w_scales{b}{a}{t0}", align_bytes=64)
+        def quant_w(g, b, a, t0, nt, slot=None):
+            codes = sb([P, nt * P], U32, f"w_codes{b}{a}{t0}", slot)
+            scales = sb([P, nt * P], U8, f"w_scales{b}{a}{t0}")
             nc.vector.quantize_mx(out=codes[:].bitcast(FP8X4), scales=scales[:], in_=g[:])
             for t in range(nt):
                 w_ops[(b, a, t0 + t)] = (codes[:, t * P : (t + 1) * P], scales[:, t * P : (t + 1) * P])
 
-        sc1 = load_scales(tab_scales, KP, 0, "sc1", nc.gpsimd)
-        sc3 = load_scales(tab3_scales, HP, 0, "sc3", nc.gpsimd)
-        sc2 = load_scales(tab2_scales, HP, 8, "sc2", nc.gpsimd)
-        w_raw = {}
-        words1 = []
-        w_raw[(0, 0)] = load_w(0, 0)
-        list1 = load_list(offs, "list1")
-        words1.append(load_words(tab_words, 0, "words1_0"))
-        w_raw[(0, 1)] = load_w(0, 1)
-        list3 = load_list(offs3, "list3")
-        list2 = load_list(offs2, "list2")
-        gain_sb = keep.tile([P, HP, PACK], F32, name="gain_sb")
-        nc.scalar.dma_start(out=gain_sb[:], in_=gain.rearrange("(b p t) -> p b t", b=HP, t=PACK))
-        low_sb = keep.tile([P, S2 // P], F32, name="low_sb")
-        with nc.allow_non_contiguous_dma(reason="one level a partition"):
-            nc.scalar.dma_start(out=low_sb[:], in_=low.rearrange("(c p) -> p c", p=P))
-        words1.append(load_words(tab_words, 1, "words1_1"))
-        w_raw[(0, 2)] = load_w(0, 2)
-        words1.append(load_words(tab_words, 2, "words1_2"))
-        res_sb = [load_res(0)]
-        for a in range(KP):
-            w_raw[(1, a)] = load_w(1, a)
-        res_sb.append(load_res(1))
-        words3 = [load_words(tab3_words, b, f"words3_{b}") for b in range(HP)]
-        words2 = [load_words(tab2_words, b, f"words2_{b}") for b in range(HP)]
-
         banks = {}
 
-        def stage1_pass(b, a, v_words, v_scales):
-            for t in range(PACK):
+        def stage1_pass(b, a, ts=range(PACK)):
+            for t in ts:
                 if a == 0:
                     banks[(b, t)] = psum.tile([P, S], F32, name=f"h_acc{b}{t}", tag=f"bank{b}{t}")
                 codes, scales = w_ops[(b, a, t)]
@@ -126,26 +103,43 @@ def tile_list_cohousing_household_scores_kernel(
                     start=(a == 0), stop=(a == KP - 1),
                 )
 
-        h_codes = [keep.tile([P, S], U32, name=f"h_codes{b}", align_bytes=64) for b in range(HP)]
-        h_scales = [keep.tile([P, S], U8, name=f"h_scales{b}", align_bytes=64) for b in range(HP)]
+        h_codes = [sb([P, S], U32, f"h_codes{b}") for b in range(HP)]
+        h_scales = [sb([P, S], U8, f"h_scales{b}") for b in range(HP)]
 
-        def h_add_tanh(b, hf):
-            cols = slice(hf * HALF, (hf + 1) * HALF)
-            x = ring.tile([P, PACK, HALF], F32, name="x")
-            for t in range(PACK):
-                nc.vector.tensor_tensor(out=x[:, t, :], in0=banks[(b, t)][:, cols], in1=res_sb[b][:, t, cols], op=ALU.add)
-            th = ring.tile([P, HALF, PACK], F32, name="th")
+        def h_add(b, ts):
+            x = sb([P, PACK, S], F32, f"x{b}", "x")
+            for t in ts:
+                nc.vector.tensor_tensor(out=x[:, t, :], in0=banks[(b, t)][:], in1=res_sb[b][:, t, :], op=ALU.add)
+            return x
+
+        def h_tanh_woven(b, hf, x):
+            th = sb([P, HALF, PACK], F32, f"th{b}{hf}", f"th{hf}")
             nc.scalar.activation(
                 out=th[:].rearrange("p (c i) t -> p c t i", i=4),
-                in_=x[:].rearrange("p t (c i) -> p c t i", i=4),
+                in_=x[:, :, hf * HALF : (hf + 1) * HALF].rearrange("p t (c i) -> p c t i", i=4),
                 func=ACT.Tanh,
             )
             return th
 
-        def h_gain(b, th):
-            hb = ring.tile([P, HALF, PACK], BF16, name="hb", align_bytes=64)
+        def h_gain_woven(b, hf, th):
+            hb = sb([P, HALF, PACK], BF16, f"hb{b}{hf}", f"hb{hf}")
             nc.vector.tensor_tensor(
                 out=hb[:], in0=th[:], in1=gain_sb[:, b : b + 1, :].broadcast_to([P, HALF, PACK]), op=ALU.mult
+            )
+            return hb
+
+        def h_tanh_gain(b, hf, x):
+            th = sb([P, PACK, HALF], F32, f"th{b}{hf}", f"th{hf}")
+            nc.scalar.activation(out=th[:], in_=x[:, :, hf * HALF : (hf + 1) * HALF], func=ACT.Tanh)
+            hp = sb([P, PACK, HALF], BF16, f"hp{b}{hf}")
+            for t in range(PACK):
+                nc.scalar.activation(out=hp[:, t, :], in_=th[:, t, :], func=ACT.Copy, scale=gain_sb[:, b, t : t + 1])
+            return hp
+
+        def h_weave(b, hf, hp):
+            hb = sb([P, HALF, PACK], BF16, f"hb{b}{hf}", f"hb{hf}")
+            nc.vector.tensor_copy(
+                out=hb[:].rearrange("p (c i) t -> p c t i", i=4), in_=hp[:].rearrange("p t (c i) -> p c t i", i=4)
             )
             return hb
 
@@ -156,66 +150,110 @@ def tile_list_cohousing_household_scores_kernel(
                 in_=hb[:].rearrange("p c t -> p (c t)"),
             )
 
-        def stage2_pass(acc, b, words, scales, row0, c, c0):
+        def stage2_pass(acc, b, words, scales, row0, c):
+            cols = slice(c * P, (c + 1) * P)
             nc.tensor.matmul_mx(
-                out=acc[:], lhsT=words[:, c0 : c0 + P].bitcast(FP8X4),
-                lhsT_scale=scales[row0 + 4 * b : P, c * P : (c + 1) * P],
+                out=acc[:], lhsT=words[:, cols].bitcast(FP8X4), lhsT_scale=scales[row0 + 4 * b : P, cols],
                 rhs=h_codes[b][:].bitcast(FP8X4), rhs_scale=h_scales[b][:],
                 start=(b == 0), stop=(b == HP - 1),
             )
 
-        v_scales = gather(sc1, list1, 0, S, U8, "v_scales")
-        v_words = []
+        w_raw, words1, res_sb = {}, [], []
+        sc1 = load_scales(tab_scales, KP, 0, "sc1")
+        sc3 = load_scales(tab3_scales, HP, 0, "sc3")
+        sc2 = load_scales(tab2_scales, HP, 8, "sc2")
+        w_raw[(0, 0)] = load_w(0, 0)
+        list1 = load_list(offs, "list1")
+        words1.append(load_words(tab_words, 0, "words1_0"))
+        w_raw[(0, 1)] = load_w(0, 1)
+        list3 = load_list(offs3, "list3")
+        list2 = load_list(offs2, "list2")
+        gain_sb = keep.tile([P, HP, PACK], F32, name="gain_sb")
+        nc.scalar.dma_start(out=gain_sb[:], in_=gain.rearrange("(b p t) -> p b t", b=HP, t=PACK))
+        low_sb = keep.tile([P, MT], F32, name="low_sb")
+        with nc.allow_non_contiguous_dma(reason="one level a partition"):
+            nc.scalar.dma_start(out=low_sb[:], in_=low.rearrange("(c p) -> p c", p=P))
+        words1.append(load_words(tab_words, 1, "words1_1"))
+        words1.append(load_words(tab_words, 2, "words1_2"))
+        w_raw[(0, 2)] = load_w(0, 2)
+        res_sb.append(load_res(0))
         for a in range(KP):
-            if a == KP - 1:
-                v3_scales = gather(sc3, list3, 0, S2, U8, "v3_scales")
-                v2_scales = gather(sc2, list2, 0, S2, U8, "v2_scales")
-            g = cast_w(w_raw[(0, a)], 0, a, 0, PACK, nc.scalar.copy)
-            v_words.append(gather(words1[a], list1, 0, S, U32, f"v_words{a}"))
-            quant_w(g, 0, a, 0, PACK)
-            stage1_pass(0, a, v_words, v_scales)
-        ths = [h_add_tanh(0, hf) for hf in range(2)]
-        g10 = cast_w(w_raw[(1, 0)], 1, 0, 0, PACK, nc.scalar.copy)
-        hbs = [h_gain(0, th) for th in ths]
-        g11 = cast_w(w_raw[(1, 1)], 1, 1, 0, PACK, nc.vector.tensor_copy)
-        for hf in range(2):
-            h_quant(0, hf, hbs[hf])
-        quant_w(g11, 1, 1, 0, PACK)
-        quant_w(g10, 1, 0, 0, PACK)
-        stage1_pass(1, 0, v_words, v_scales)
-        stage1_pass(1, 1, v_words, v_scales)
-        g12a = cast_w(w_raw[(1, 2)], 1, 2, 0, 2, nc.scalar.copy)
-        g12b = cast_w(w_raw[(1, 2)], 1, 2, 2, 2, nc.vector.tensor_copy)
-        quant_w(g12a, 1, 2, 0, 2)
-        quant_w(g12b, 1, 2, 2, 2)
-        stage1_pass(1, 2, v_words, v_scales)
-        ths = [h_add_tanh(1, hf) for hf in range(2)]
+            w_raw[(1, a)] = load_w(1, a)
+        res_sb.append(load_res(1))
+        words3 = [load_words(tab3_words, b, f"words3_{b}") for b in range(HP)]
+        words2 = [load_words(tab2_words, b, f"words2_{b}") for b in range(HP)]
 
-        MT = S2 // P
+        v_words = []
+        g00 = cast_w(0, 0, 0, PACK, nc.scalar.copy)
+        v_words.append(gather(words1[0], list1, U32, "v_words0"))
+        quant_w(g00, 0, 0, 0, PACK)
+        v_scales = gather(sc1, list1, U8, "v_scales", "words1_0")
+        stage1_pass(0, 0)
+        g01 = cast_w(0, 1, 0, PACK, nc.scalar.copy, "w_raw00")
+        v3_scales = gather(sc3, list3, U8, "v3_scales", "w_bf000")
+        v_words.append(gather(words1[1], list1, U32, "v_words1", "sc1"))
+        quant_w(g01, 0, 1, 0, PACK, "sc3")
+        stage1_pass(0, 1)
+        v_words.append(gather(words1[2], list1, U32, "v_words2", "words1_1"))
+        g02a = cast_w(0, 2, 0, 2, nc.scalar.copy, "w_raw01")
+        g02b = cast_w(0, 2, 2, 2, nc.vector.tensor_copy, "w_raw00")
+        quant_w(g02b, 0, 2, 2, 2)
+        quant_w(g02a, 0, 2, 0, 2)
+        stage1_pass(0, 2, (2, 3, 0, 1))
+        v2_scales = gather(sc2, list2, U8, "v2_scales", "w_raw00")
+        g10a = cast_w(1, 0, 0, 2, nc.scalar.copy, "w_raw02")
+        x = h_add(0, (2, 3, 0, 1))
+        ths = [h_tanh_woven(0, hf, x) for hf in range(2)]
+        g10b = cast_w(1, 0, 2, 2, nc.scalar.copy, "x")
+        g11a = cast_w(1, 1, 0, 2, nc.scalar.copy, "w_raw10")
+        quant_w(g10a, 1, 0, 0, 2, "res0")
+        hb0 = h_gain_woven(0, 0, ths[0])
+        g11b = cast_w(1, 1, 2, 2, nc.vector.tensor_copy, "w_raw02")
+        hb1 = h_gain_woven(0, 1, ths[1])
+        g12b = cast_w(1, 2, 2, 2, nc.vector.tensor_copy, "th0")
+        g12a = cast_w(1, 2, 0, 2, nc.scalar.copy, "w_raw11")
+        quant_w(g11b, 1, 1, 2, 2)
+        quant_w(g10b, 1, 0, 2, 2)
+        quant_w(g12b, 1, 2, 2, 2)
+        quant_w(g11a, 1, 1, 0, 2)
+        h_quant(0, 0, hb0)
+        quant_w(g12a, 1, 2, 0, 2)
+        h_quant(0, 1, hb1)
+        stage1_pass(1, 0, (0, 1))
+        for a in range(KP):
+            stage1_pass(1, a, (2, 3))
+        for a in range(1, KP):
+            stage1_pass(1, a, (0, 1))
+        x = h_add(1, (2, 3, 0, 1))
+        th0 = h_tanh_woven(1, 0, x)
+        hp1 = h_tanh_gain(1, 1, x)
+
         e3 = [psum.tile([P, S], F32, name=f"e3_{c}", tag=f"bank0{c}") for c in range(MT)]
         e2 = [psum.tile([P, S], F32, name=f"e2_{c}", tag=f"bank1{c}") for c in range(MT)]
-        g3 = gather(words3[0], list3, 0, S2, U32, "v3_words0")
+        g3 = gather(words3[0], list3, U32, "v3_words0", "res1")
         for c in range(MT):
-            stage2_pass(e3[c], 0, g3, v3_scales, 0, c, c * P)
-        hbs = [h_gain(1, th) for th in ths]
-        g3 = gather(words3[1], list3, 0, S2, U32, "v3_words1")
-        for hf in range(2):
-            h_quant(1, hf, hbs[hf])
+            stage2_pass(e3[c], 0, g3, v3_scales, 0, c)
+        hb0 = h_gain_woven(1, 0, th0)
+        g3 = gather(words3[1], list3, U32, "v3_words1", "words3_0")
+        h_quant(1, 0, hb0)
+        hb1 = h_weave(1, 1, hp1)
+        h_quant(1, 1, hb1)
+        g2 = gather(words2[0], list2, U32, "v2_words0", "hp11")
         for c in range(MT):
-            stage2_pass(e3[c], 1, g3, v3_scales, 0, c, c * P)
+            stage2_pass(e3[c], 1, g3, v3_scales, 0, c)
         th3 = []
         for c in range(MT):
-            t3 = keep.tile([P, S], F32, name=f"th3_{c}")
+            t3 = sb([P, S], F32, f"th3_{c}")
             nc.scalar.activation(out=t3[:], in_=e3[c][:], func=ACT.Tanh)
             th3.append(t3)
-        g2 = gather(words2[0], list2, 0, S2, U32, "v2_words0")
         for c in range(MT):
-            stage2_pass(e2[c], 0, g2, v2_scales, 8, c, c * P)
+            stage2_pass(e2[c], 0, g2, v2_scales, 8, c)
+        g2 = sb([P, S2], U32, "v2_words1", "hb1")
         for c in range(MT):
-            g2c = gather(words2[1], list2, c * P, P, U32, f"v2_words1_{c}")
-            stage2_pass(e2[c], 1, g2c, v2_scales, 8, c, 0)
+            nc.vector.tensor_copy(out=g2[:, c * P : (c + 1) * P], in_=words2[1][:].indirect(list2[:, c * P // 16 : (c + 1) * P // 16]))
+            stage2_pass(e2[c], 1, g2, v2_scales, 8, c)
         for c in range(MT):
-            o = keep.tile([P, S], F32, name=f"o{c}")
+            o = sb([P, S], F32, f"o{c}")
             nc.vector.scalar_tensor_tensor(
                 out=o[:], in0=e2[c][:], scalar=low_sb[:, c : c + 1], in1=th3[c][:], op0=ALU.max, op1=ALU.mult
             )

@@ -42,16 +42,16 @@ def tile_list_cohousing_household_scores_kernel(
             nc.sync.dma_start(t[:], src)
             return t
 
-        def load_words(words, a, name):
-            t = sb([P, T], U32, name)
+        def load_words(words, a, name, slot=None):
+            t = sb([P, T], U32, name, slot)
             nc.sync.dma_start(out=t[:].bitcast(I32), in_=words[a].rearrange("p n t -> p (n t)").bitcast(I32))
             return t
 
-        def load_scales(scales, passes, row0, name):
+        def load_scales(scales, passes, row0, name, queue):
             t = sb([P, T], U8, name)
             nc.vector.memset(t[:].bitcast(I32), 0)
             for q in range(4):
-                nc.gpsimd.dma_start(
+                queue.dma_start(
                     out=t[32 * q + row0 : 32 * q + row0 + 4 * passes, :].bitcast(I32),
                     in_=scales[:, 4 * q : 4 * q + 4, :].bitcast(I32),
                 )
@@ -62,14 +62,13 @@ def tile_list_cohousing_household_scores_kernel(
             nc.vector.tensor_copy(out=g[:], in_=window[:].indirect(lst[:]))
             return g
 
-        def load_w(b, a):
-            t = sb([P, PACK, K_PASS], F32, f"w_raw{b}{a}")
-            rows = w1[a * K_PASS : (a + 1) * K_PASS, b * K_PASS : (b + 1) * K_PASS]
-            nc.sync.dma_start(out=t[:], in_=rows.rearrange("(p j) c -> p j c", j=PACK))
+        def load_w(a):
+            t = sb([P, PACK, H], F32, f"w_raw{a}")
+            nc.sync.dma_start(out=t[:], in_=w1[a * K_PASS : (a + 1) * K_PASS, :].rearrange("(p j) c -> p j c", j=PACK))
             return t
 
-        def load_res(b):
-            t = sb([P, PACK, S], F32, f"res{b}")
+        def load_res(b, slot=None):
+            t = sb([P, PACK, S], F32, f"res{b}", slot)
             nc.sync.dma_start(out=t[:], in_=res[b * K_PASS : (b + 1) * K_PASS, :].rearrange("(p t) j -> p t j", t=PACK))
             return t
 
@@ -79,7 +78,7 @@ def tile_list_cohousing_household_scores_kernel(
             g = sb([P, nt * K_PASS], BF16, f"w_bf{b}{a}{t0}", slot)
             copy(
                 out=g[:].rearrange("p (t m j) -> p m j t", t=nt, j=PACK),
-                in_=w_raw[(b, a)][:].rearrange("p j (m t) -> p m j t", t=PACK)[:, :, :, t0 : t0 + nt],
+                in_=w_raw[a][:, :, b * K_PASS : (b + 1) * K_PASS].rearrange("p j (m t) -> p m j t", t=PACK)[:, :, :, t0 : t0 + nt],
             )
             return g
 
@@ -106,9 +105,9 @@ def tile_list_cohousing_household_scores_kernel(
         h_codes = [sb([P, S], U32, f"h_codes{b}") for b in range(HP)]
         h_scales = [sb([P, S], U8, f"h_scales{b}") for b in range(HP)]
 
-        def h_add(b, ts):
-            x = sb([P, PACK, S], F32, f"x{b}", "x")
-            for t in ts:
+        def h_add(b, slot):
+            x = sb([P, PACK, S], F32, f"x{b}", slot)
+            for t in range(PACK):
                 nc.vector.tensor_tensor(out=x[:, t, :], in0=banks[(b, t)][:], in1=res_sb[b][:, t, :], op=ALU.add)
             return x
 
@@ -128,17 +127,20 @@ def tile_list_cohousing_household_scores_kernel(
             )
             return hb
 
-        def h_tanh_gain(b, hf, x):
+        def h_tanh(b, hf, x):
             th = sb([P, PACK, HALF], F32, f"th{b}{hf}", f"th{hf}")
             nc.scalar.activation(out=th[:], in_=x[:, :, hf * HALF : (hf + 1) * HALF], func=ACT.Tanh)
-            hp = sb([P, PACK, HALF], BF16, f"hp{b}{hf}")
+            return th
+
+        def h_gain(b, hf, th, slot=None):
+            hp = sb([P, PACK, HALF], BF16, f"hp{b}{hf}", slot)
             for t in range(PACK):
                 nc.scalar.activation(out=hp[:, t, :], in_=th[:, t, :], func=ACT.Copy, scale=gain_sb[:, b, t : t + 1])
             return hp
 
         def h_weave(b, hf, hp):
-            hb = sb([P, HALF, PACK], BF16, f"hb{b}{hf}", f"hb{hf}")
-            nc.vector.tensor_copy(
+            hb = sb([P, HALF, PACK], BF16, f"hb{b}{hf}")
+            nc.scalar.copy(
                 out=hb[:].rearrange("p (c i) t -> p c t i", i=4), in_=hp[:].rearrange("p t (c i) -> p c t i", i=4)
             )
             return hb
@@ -150,22 +152,20 @@ def tile_list_cohousing_household_scores_kernel(
                 in_=hb[:].rearrange("p c t -> p (c t)"),
             )
 
-        def stage2_pass(acc, b, words, scales, row0, c):
+        def stage2_pass(acc, b, words, scales, row0, c, j0=0, j1=S):
             cols = slice(c * P, (c + 1) * P)
             nc.tensor.matmul_mx(
-                out=acc[:], lhsT=words[:, cols].bitcast(FP8X4), lhsT_scale=scales[row0 + 4 * b : P, cols],
-                rhs=h_codes[b][:].bitcast(FP8X4), rhs_scale=h_scales[b][:],
-                start=(b == 0), stop=(b == HP - 1),
+                out=acc[:, j0:j1], lhsT=words[:, cols].bitcast(FP8X4), lhsT_scale=scales[row0 + 4 * b : P, cols],
+                rhs=h_codes[b][:, j0:j1].bitcast(FP8X4), rhs_scale=h_scales[b][:, j0:j1],
+                start=(b == 0), stop=(b == HP - 1 and j1 == S),
             )
 
-        w_raw, words1, res_sb = {}, [], []
-        sc1 = load_scales(tab_scales, KP, 0, "sc1")
-        sc3 = load_scales(tab3_scales, HP, 0, "sc3")
-        sc2 = load_scales(tab2_scales, HP, 8, "sc2")
-        w_raw[(0, 0)] = load_w(0, 0)
+        sc1 = load_scales(tab_scales, KP, 0, "sc1", nc.gpsimd)
+        sc3 = load_scales(tab3_scales, HP, 0, "sc3", nc.gpsimd)
+        sc2 = load_scales(tab2_scales, HP, 8, "sc2", nc.gpsimd)
+        w_raw = [load_w(0)]
         list1 = load_list(offs, "list1")
-        words1.append(load_words(tab_words, 0, "words1_0"))
-        w_raw[(0, 1)] = load_w(0, 1)
+        words1 = [load_words(tab_words, 0, "words1_0")]
         list3 = load_list(offs3, "list3")
         list2 = load_list(offs2, "list2")
         gain_sb = keep.tile([P, HP, PACK], F32, name="gain_sb")
@@ -173,82 +173,71 @@ def tile_list_cohousing_household_scores_kernel(
         low_sb = keep.tile([P, MT], F32, name="low_sb")
         with nc.allow_non_contiguous_dma(reason="one level a partition"):
             nc.scalar.dma_start(out=low_sb[:], in_=low.rearrange("(c p) -> p c", p=P))
+        w_raw.append(load_w(1))
         words1.append(load_words(tab_words, 1, "words1_1"))
+        w_raw.append(load_w(2))
         words1.append(load_words(tab_words, 2, "words1_2"))
-        w_raw[(0, 2)] = load_w(0, 2)
-        res_sb.append(load_res(0))
-        for a in range(KP):
-            w_raw[(1, a)] = load_w(1, a)
-        res_sb.append(load_res(1))
-        words3 = [load_words(tab3_words, b, f"words3_{b}") for b in range(HP)]
-        words2 = [load_words(tab2_words, b, f"words2_{b}") for b in range(HP)]
+        res_sb = [load_res(b) for b in range(HP)]
+        words3, words2 = [], []
+        for b in range(HP):
+            words3.append(load_words(tab3_words, b, f"words3_{b}"))
+            words2.append(load_words(tab2_words, b, f"words2_{b}"))
 
         v_words = []
-        g00 = cast_w(0, 0, 0, PACK, nc.scalar.copy)
-        v_words.append(gather(words1[0], list1, U32, "v_words0"))
-        quant_w(g00, 0, 0, 0, PACK)
+        g0 = cast_w(0, 0, 0, PACK, nc.scalar.copy)
+        g1 = cast_w(1, 0, 0, PACK, nc.vector.tensor_copy)
+        quant_w(g1, 1, 0, 0, PACK)
+        v_words.append(gather(words1[0], list1, U32, "v_words0", "w_bf100"))
+        quant_w(g0, 0, 0, 0, PACK)
         v_scales = gather(sc1, list1, U8, "v_scales", "words1_0")
+        stage1_pass(1, 0)
         stage1_pass(0, 0)
-        g01 = cast_w(0, 1, 0, PACK, nc.scalar.copy, "w_raw00")
-        v3_scales = gather(sc3, list3, U8, "v3_scales", "w_bf000")
+        g0 = cast_w(0, 1, 0, PACK, nc.scalar.copy, "w_raw0")
+        g1 = cast_w(1, 1, 0, PACK, nc.vector.tensor_copy, "sc1")
+        quant_w(g1, 1, 1, 0, PACK)
         v_words.append(gather(words1[1], list1, U32, "v_words1", "sc1"))
-        quant_w(g01, 0, 1, 0, PACK, "sc3")
+        quant_w(g0, 0, 1, 0, PACK)
+        stage1_pass(1, 1)
         stage1_pass(0, 1)
-        v_words.append(gather(words1[2], list1, U32, "v_words2", "words1_1"))
-        g02a = cast_w(0, 2, 0, 2, nc.scalar.copy, "w_raw01")
-        g02b = cast_w(0, 2, 2, 2, nc.vector.tensor_copy, "w_raw00")
-        quant_w(g02b, 0, 2, 2, 2)
-        quant_w(g02a, 0, 2, 0, 2)
-        stage1_pass(0, 2, (2, 3, 0, 1))
-        v2_scales = gather(sc2, list2, U8, "v2_scales", "w_raw00")
-        g10a = cast_w(1, 0, 0, 2, nc.scalar.copy, "w_raw02")
-        x = h_add(0, (2, 3, 0, 1))
-        ths = [h_tanh_woven(0, hf, x) for hf in range(2)]
-        g10b = cast_w(1, 0, 2, 2, nc.scalar.copy, "x")
-        g11a = cast_w(1, 1, 0, 2, nc.scalar.copy, "w_raw10")
-        quant_w(g10a, 1, 0, 0, 2, "res0")
-        hb0 = h_gain_woven(0, 0, ths[0])
-        g11b = cast_w(1, 1, 2, 2, nc.vector.tensor_copy, "w_raw02")
-        hb1 = h_gain_woven(0, 1, ths[1])
-        g12b = cast_w(1, 2, 2, 2, nc.vector.tensor_copy, "th0")
-        g12a = cast_w(1, 2, 0, 2, nc.scalar.copy, "w_raw11")
-        quant_w(g11b, 1, 1, 2, 2)
-        quant_w(g10b, 1, 0, 2, 2)
-        quant_w(g12b, 1, 2, 2, 2)
-        quant_w(g11a, 1, 1, 0, 2)
-        h_quant(0, 0, hb0)
-        quant_w(g12a, 1, 2, 0, 2)
-        h_quant(0, 1, hb1)
-        stage1_pass(1, 0, (0, 1))
-        for a in range(KP):
-            stage1_pass(1, a, (2, 3))
-        for a in range(1, KP):
-            stage1_pass(1, a, (0, 1))
-        x = h_add(1, (2, 3, 0, 1))
-        th0 = h_tanh_woven(1, 0, x)
-        hp1 = h_tanh_gain(1, 1, x)
-
+        v3_scales = gather(sc3, list3, U8, "v3_scales", "words1_1")
+        v2_scales = gather(sc2, list2, U8, "v2_scales", "sc3")
+        g0 = cast_w(0, 2, 0, PACK, nc.vector.tensor_copy, "sc2")
+        g1 = cast_w(1, 2, 0, PACK, nc.scalar.copy, "w_raw1")
+        quant_w(g0, 0, 2, 0, PACK)
+        v_words.append(gather(words1[2], list1, U32, "v_words2", "sc2"))
+        stage1_pass(0, 2)
+        quant_w(g1, 1, 2, 0, PACK)
+        stage1_pass(1, 2)
+        x0 = h_add(0, "w_raw0")
+        x1 = h_add(1, "w_raw1")
+        th0 = h_tanh_woven(0, 0, x0)
+        hb1 = h_weave(0, 1, h_gain(0, 1, h_tanh(0, 1, x0)))
+        hb0 = h_gain_woven(0, 0, th0)
         e3 = [psum.tile([P, S], F32, name=f"e3_{c}", tag=f"bank0{c}") for c in range(MT)]
         e2 = [psum.tile([P, S], F32, name=f"e2_{c}", tag=f"bank1{c}") for c in range(MT)]
         g3 = gather(words3[0], list3, U32, "v3_words0", "res1")
+        h_quant(0, 0, hb0)
+        h_quant(0, 1, hb1)
         for c in range(MT):
             stage2_pass(e3[c], 0, g3, v3_scales, 0, c)
-        hb0 = h_gain_woven(1, 0, th0)
-        g3 = gather(words3[1], list3, U32, "v3_words1", "words3_0")
-        h_quant(1, 0, hb0)
-        hb1 = h_weave(1, 1, hp1)
-        h_quant(1, 1, hb1)
-        g2 = gather(words2[0], list2, U32, "v2_words0", "hp11")
+        th0 = h_tanh_woven(1, 0, x1)
+        hb1 = h_weave(1, 1, h_gain(1, 1, h_tanh(1, 1, x1)))
+        g2 = gather(words2[0], list2, U32, "v2_words0", "hb01")
         for c in range(MT):
-            stage2_pass(e3[c], 1, g3, v3_scales, 0, c)
+            stage2_pass(e2[c], 0, g2, v2_scales, 8, c)
+        hb0 = h_gain_woven(1, 0, th0)
+        g3 = gather(words3[1], list3, U32, "v3_words1", "th0")
+        h_quant(1, 0, hb0)
+        for c in range(MT):
+            stage2_pass(e3[c], 1, g3, v3_scales, 0, c, 0, HALF)
+        h_quant(1, 1, hb1)
+        g2 = sb([P, S2], U32, "v2_words1", "hb11")
         th3 = []
         for c in range(MT):
+            stage2_pass(e3[c], 1, g3, v3_scales, 0, c, HALF, S)
             t3 = sb([P, S], F32, f"th3_{c}")
             nc.scalar.activation(out=t3[:], in_=e3[c][:], func=ACT.Tanh)
             th3.append(t3)
-        for c in range(MT):
-            stage2_pass(e2[c], 0, g2, v2_scales, 8, c)
-        g2 = sb([P, S2], U32, "v2_words1", "hb1")
         for c in range(MT):
             nc.vector.tensor_copy(out=g2[:, c * P : (c + 1) * P], in_=words2[1][:].indirect(list2[:, c * P // 16 : (c + 1) * P // 16]))
             stage2_pass(e2[c], 1, g2, v2_scales, 8, c)

@@ -106,16 +106,18 @@ def tile_list_cohousing_household_scores_kernel(
         h_scales = [sb([P, S], U8, f"h_scales{b}") for b in range(HP)]
 
         def h_add(b, slot):
-            x = sb([P, PACK, S], F32, f"x{b}", slot)
-            for t in range(PACK):
-                nc.vector.tensor_tensor(out=x[:, t, :], in0=banks[(b, t)][:], in1=res_sb[b][:, t, :], op=ALU.add)
+            x = sb([P, 2, PACK, HALF], F32, f"x{b}", slot)
+            for hf in range(2):
+                cols = slice(hf * HALF, (hf + 1) * HALF)
+                for t in range(PACK):
+                    nc.vector.tensor_tensor(out=x[:, hf, t, :], in0=banks[(b, t)][:, cols], in1=res_sb[b][:, t, cols], op=ALU.add)
             return x
 
         def h_tanh_woven(b, hf, x):
             th = sb([P, HALF, PACK], F32, f"th{b}{hf}", f"th{hf}")
             nc.scalar.activation(
                 out=th[:].rearrange("p (c i) t -> p c t i", i=4),
-                in_=x[:, :, hf * HALF : (hf + 1) * HALF].rearrange("p t (c i) -> p c t i", i=4),
+                in_=x[:, hf, :, :].rearrange("p t (c i) -> p c t i", i=4),
                 func=ACT.Tanh,
             )
             return th
@@ -129,7 +131,7 @@ def tile_list_cohousing_household_scores_kernel(
 
         def h_tanh(b, hf, x):
             th = sb([P, PACK, HALF], F32, f"th{b}{hf}", f"th{hf}")
-            nc.scalar.activation(out=th[:], in_=x[:, :, hf * HALF : (hf + 1) * HALF], func=ACT.Tanh)
+            nc.scalar.activation(out=th[:], in_=x[:, hf, :, :], func=ACT.Tanh)
             return th
 
         def h_gain(b, hf, th, slot=None):
@@ -200,16 +202,16 @@ def tile_list_cohousing_household_scores_kernel(
         stage1_pass(1, 1)
         stage1_pass(0, 1)
         v3_scales = gather(sc3, list3, U8, "v3_scales", "words1_1")
-        v2_scales = gather(sc2, list2, U8, "v2_scales", "sc3")
-        g0 = cast_w(0, 2, 0, PACK, nc.vector.tensor_copy, "sc2")
+        g0 = cast_w(0, 2, 0, PACK, nc.vector.tensor_copy, "sc3")
         g1 = cast_w(1, 2, 0, PACK, nc.scalar.copy, "w_raw1")
         quant_w(g0, 0, 2, 0, PACK)
-        v_words.append(gather(words1[2], list1, U32, "v_words2", "sc2"))
+        v_words.append(gather(words1[2], list1, U32, "v_words2", "sc3"))
         stage1_pass(0, 2)
         quant_w(g1, 1, 2, 0, PACK)
         stage1_pass(1, 2)
-        x0 = h_add(0, "w_raw0")
-        x1 = h_add(1, "w_raw1")
+        v2_scales = gather(sc2, list2, U8, "v2_scales", "w_raw1")
+        x0 = h_add(0, "sc2")
+        x1 = h_add(1, "res0")
         th0 = h_tanh_woven(0, 0, x0)
         hb1 = h_weave(0, 1, h_gain(0, 1, h_tanh(0, 1, x0)))
         hb0 = h_gain_woven(0, 0, th0)
@@ -241,9 +243,10 @@ def tile_list_cohousing_household_scores_kernel(
         for c in range(MT):
             nc.vector.tensor_copy(out=g2[:, c * P : (c + 1) * P], in_=words2[1][:].indirect(list2[:, c * P // 16 : (c + 1) * P // 16]))
             stage2_pass(e2[c], 1, g2, v2_scales, 8, c)
-        for c in range(MT):
-            o = sb([P, S], F32, f"o{c}")
+        pieces = [(c, 0, S) for c in range(MT - 1)] + [(MT - 1, 0, HALF), (MT - 1, HALF, S)]
+        for c, j0, j1 in pieces:
+            o = sb([P, j1 - j0], F32, f"o{c}_{j0}")
             nc.vector.scalar_tensor_tensor(
-                out=o[:], in0=e2[c][:], scalar=low_sb[:, c : c + 1], in1=th3[c][:], op0=ALU.max, op1=ALU.mult
+                out=o[:], in0=e2[c][:, j0:j1], scalar=low_sb[:, c : c + 1], in1=th3[c][:, j0:j1], op0=ALU.max, op1=ALU.mult
             )
-            nc.sync.dma_start(out=out[c * P : (c + 1) * P, :], in_=o[:])
+            nc.sync.dma_start(out=out[c * P : (c + 1) * P, j0:j1], in_=o[:])

from contextlib import ExitStack

import concourse.mybir as mybir

K, T, S, H, T3, S2 = 1536, 2048, 512, 1024, 2048, 512
FLOPS = 2 * K * H * S + 2 * 2 * H * S2 * S

F32 = mybir.dt.float32
BF16 = mybir.dt.bfloat16
I32 = mybir.dt.int32
U32 = mybir.dt.uint32
U16 = mybir.dt.uint16
U8 = mybir.dt.uint8
FP8X4 = mybir.dt.float8_e4m3fn_x4
ALU = mybir.AluOpType
ACT = mybir.ActivationFunctionType

P = 128
PACK = 4
K_PASS = P * PACK
KP = K // K_PASS
HP = H // K_PASS
HALF = S // 2
MT = S2 // P


def tile_list_cohousing_household_scores_kernel(
    tc, tab_words, tab_scales, offs, tab2_words, tab2_scales, offs2,
    tab3_words, tab3_scales, offs3, w1, res, gain, low, out,
):
    nc = tc.nc
    with ExitStack() as ctx:
        lists = ctx.enter_context(tc.tile_pool(name="lists", bufs=1))
        keep = ctx.enter_context(tc.tile_pool(name="keep", bufs=1))
        psum = ctx.enter_context(tc.psum_pool(name="psum", bufs=1))

        def sb(shape, dtype, name, slot=None):
            return keep.tile(shape, dtype, name=name, tag=slot or name, align_bytes=64)

        def load_list(src, name):
            t = lists.tile([P, S // 16], U16, name=name)
            nc.sync.dma_start(t[:], src)
            return t

        def load_words(words, a, name, slot=None):
            t = sb([P, T], U32, name, slot)
            nc.sync.dma_start(out=t[:].bitcast(I32), in_=words[a].rearrange("p n t -> p (n t)").bitcast(I32))
            return t

        def load_scales(scales, passes, row0, name, queue):
            t = sb([P, T], U8, name)
            nc.vector.memset(t[:].bitcast(I32), 0)
            for q in range(4):
                queue.dma_start(
                    out=t[32 * q + row0 : 32 * q + row0 + 4 * passes, :].bitcast(I32),
                    in_=scales[:, 4 * q : 4 * q + 4, :].bitcast(I32),
                )
            return t

        def gather(window, lst, dtype, name, slot=None):
            g = sb([P, S], dtype, name, slot)
            nc.vector.tensor_copy(out=g[:], in_=window[:].indirect(lst[:]))
            return g

        def load_w(a):
            t = sb([P, PACK, H], F32, f"w_raw{a}")
            nc.sync.dma_start(out=t[:], in_=w1[a * K_PASS : (a + 1) * K_PASS, :].rearrange("(p j) c -> p j c", j=PACK))
            return t

        def load_res(b, slot=None):
            t = sb([P, PACK, S], F32, f"res{b}", slot)
            nc.sync.dma_start(out=t[:], in_=res[b * K_PASS : (b + 1) * K_PASS, :].rearrange("(p t) j -> p t j", t=PACK))
            return t

        w_ops = {}

        def cast_w(b, a, t0, nt, copy, slot=None):
            g = sb([P, nt * K_PASS], BF16, f"w_bf{b}{a}{t0}", slot)
            copy(
                out=g[:].rearrange("p (t m j) -> p m j t", t=nt, j=PACK),
                in_=w_raw[a][:, :, b * K_PASS : (b + 1) * K_PASS].rearrange("p j (m t) -> p m j t", t=PACK)[:, :, :, t0 : t0 + nt],
            )
            return g

        def quant_w(g, b, a, t0, nt, slot=None):
            codes = sb([P, nt * P], U32, f"w_codes{b}{a}{t0}", slot)
            scales = sb([P, nt * P], U8, f"w_scales{b}{a}{t0}")
            nc.vector.quantize_mx(out=codes[:].bitcast(FP8X4), scales=scales[:], in_=g[:])
            for t in range(nt):
                w_ops[(b, a, t0 + t)] = (codes[:, t * P : (t + 1) * P], scales[:, t * P : (t + 1) * P])

        banks = {}

        def stage1_pass(b, a, ts=range(PACK)):
            for t in ts:
                if a == 0:
                    banks[(b, t)] = psum.tile([P, S], F32, name=f"h_acc{b}{t}", tag=f"bank{b}{t}")
                codes, scales = w_ops[(b, a, t)]
                nc.tensor.matmul_mx(
                    out=banks[(b, t)][:], lhsT=codes.bitcast(FP8X4), lhsT_scale=scales,
                    rhs=v_words[a][:].bitcast(FP8X4), rhs_scale=v_scales[4 * a : P, :],
                    start=(a == 0), stop=(a == KP - 1),
                )

        h_codes = [sb([P, S], U32, f"h_codes{b}") for b in range(HP)]
        h_scales = [sb([P, S], U8, f"h_scales{b}") for b in range(HP)]

        def h_add(b, slot):
            x = sb([P, 2, PACK, HALF], F32, f"x{b}", slot)
            for hf in range(2):
                cols = slice(hf * HALF, (hf + 1) * HALF)
                for t in range(PACK):
                    nc.vector.tensor_tensor(out=x[:, hf, t, :], in0=banks[(b, t)][:, cols], in1=res_sb[b][:, t, cols], op=ALU.add)
            return x

        def h_tanh_woven(b, hf, x):
            th = sb([P, HALF, PACK], F32, f"th{b}{hf}", f"th{hf}")
            nc.scalar.activation(
                out=th[:].rearrange("p (c i) t -> p c t i", i=4),
                in_=x[:, hf, :, :].rearrange("p t (c i) -> p c t i", i=4),
                func=ACT.Tanh,
            )
            return th

        def h_gain_woven(b, hf, th):
            hb = sb([P, HALF, PACK], BF16, f"hb{b}{hf}", f"hb{hf}")
            nc.vector.tensor_tensor(
                out=hb[:], in0=th[:], in1=gain_sb[:, b : b + 1, :].broadcast_to([P, HALF, PACK]), op=ALU.mult
            )
            return hb

        def h_tanh(b, hf, x):
            th = sb([P, PACK, HALF], F32, f"th{b}{hf}", f"th{hf}")
            nc.scalar.activation(out=th[:], in_=x[:, hf, :, :], func=ACT.Tanh)
            return th

        def h_gain(b, hf, th, slot=None):
            hp = sb([P, PACK, HALF], BF16, f"hp{b}{hf}", slot)
            for t in range(PACK):
                nc.scalar.activation(out=hp[:, t, :], in_=th[:, t, :], func=ACT.Copy, scale=gain_sb[:, b, t : t + 1])
            return hp

        def h_weave(b, hf, hp):
            hb = sb([P, HALF, PACK], BF16, f"hb{b}{hf}")
            nc.scalar.copy(
                out=hb[:].rearrange("p (c i) t -> p c t i", i=4), in_=hp[:].rearrange("p t (c i) -> p c t i", i=4)
            )
            return hb

        def h_quant(b, hf, hb):
            cols = slice(hf * HALF, (hf + 1) * HALF)
            nc.vector.quantize_mx(
                out=h_codes[b][:, cols].bitcast(FP8X4), scales=h_scales[b][:, cols],
                in_=hb[:].rearrange("p c t -> p (c t)"),
            )

        def stage2_pass(acc, b, words, scales, row0, c, j0=0, j1=S):
            cols = slice(c * P, (c + 1) * P)
            nc.tensor.matmul_mx(
                out=acc[:, j0:j1], lhsT=words[:, cols].bitcast(FP8X4), lhsT_scale=scales[row0 + 4 * b : P, cols],
                rhs=h_codes[b][:, j0:j1].bitcast(FP8X4), rhs_scale=h_scales[b][:, j0:j1],
                start=(b == 0), stop=(b == HP - 1 and j1 == S),
            )

        sc1 = load_scales(tab_scales, KP, 0, "sc1", nc.gpsimd)
        sc3 = load_scales(tab3_scales, HP, 0, "sc3", nc.gpsimd)
        sc2 = load_scales(tab2_scales, HP, 8, "sc2", nc.gpsimd)
        w_raw = [load_w(0)]
        list1 = load_list(offs, "list1")
        words1 = [load_words(tab_words, 0, "words1_0")]
        list3 = load_list(offs3, "list3")
        list2 = load_list(offs2, "list2")
        gain_sb = keep.tile([P, HP, PACK], F32, name="gain_sb")
        nc.scalar.dma_start(out=gain_sb[:], in_=gain.rearrange("(b p t) -> p b t", b=HP, t=PACK))
        low_sb = keep.tile([P, MT], F32, name="low_sb")
        with nc.allow_non_contiguous_dma(reason="one level a partition"):
            nc.scalar.dma_start(out=low_sb[:], in_=low.rearrange("(c p) -> p c", p=P))
        w_raw.append(load_w(1))
        words1.append(load_words(tab_words, 1, "words1_1"))
        w_raw.append(load_w(2))
        words1.append(load_words(tab_words, 2, "words1_2"))
        res_sb = [load_res(b) for b in range(HP)]
        words3, words2 = [], []
        for b in range(HP):
            words3.append(load_words(tab3_words, b, f"words3_{b}"))
            words2.append(load_words(tab2_words, b, f"words2_{b}"))

        v_words = []
        g0 = cast_w(0, 0, 0, PACK, nc.scalar.copy)
        g1 = cast_w(1, 0, 0, PACK, nc.vector.tensor_copy)
        quant_w(g1, 1, 0, 0, PACK)
        v_words.append(gather(words1[0], list1, U32, "v_words0", "w_bf100"))
        quant_w(g0, 0, 0, 0, PACK)
        v_scales = gather(sc1, list1, U8, "v_scales", "words1_0")
        stage1_pass(1, 0)
        stage1_pass(0, 0)
        g0 = cast_w(0, 1, 0, PACK, nc.scalar.copy, "w_raw0")
        g1 = cast_w(1, 1, 0, PACK, nc.vector.tensor_copy, "sc1")
        quant_w(g1, 1, 1, 0, PACK)
        v_words.append(gather(words1[1], list1, U32, "v_words1", "sc1"))
        quant_w(g0, 0, 1, 0, PACK)
        stage1_pass(1, 1)
        stage1_pass(0, 1)
        v3_scales = gather(sc3, list3, U8, "v3_scales", "words1_1")
        g0 = cast_w(0, 2, 0, PACK, nc.vector.tensor_copy, "sc3")
        g1 = cast_w(1, 2, 0, PACK, nc.scalar.copy, "w_raw1")
        quant_w(g0, 0, 2, 0, PACK)
        v_words.append(gather(words1[2], list1, U32, "v_words2", "sc3"))
        stage1_pass(0, 2)
        quant_w(g1, 1, 2, 0, PACK)
        stage1_pass(1, 2)
        v2_scales = gather(sc2, list2, U8, "v2_scales", "w_raw1")
        x0 = h_add(0, "sc2")
        x1 = h_add(1, "res0")
        th0 = h_tanh_woven(0, 0, x0)
        hb1 = h_weave(0, 1, h_gain(0, 1, h_tanh(0, 1, x0)))
        hb0 = h_gain_woven(0, 0, th0)
        e3 = [psum.tile([P, S], F32, name=f"e3_{c}", tag=f"bank0{c}") for c in range(MT)]
        e2 = [psum.tile([P, S], F32, name=f"e2_{c}", tag=f"bank1{c}") for c in range(MT)]
        g3 = gather(words3[0], list3, U32, "v3_words0", "res1")
        h_quant(0, 0, hb0)
        h_quant(0, 1, hb1)
        for c in range(MT):
            stage2_pass(e3[c], 0, g3, v3_scales, 0, c)
        th0 = h_tanh_woven(1, 0, x1)
        hb1 = h_weave(1, 1, h_gain(1, 1, h_tanh(1, 1, x1)))
        g2 = gather(words2[0], list2, U32, "v2_words0", "hb01")
        for c in range(MT):
            stage2_pass(e2[c], 0, g2, v2_scales, 8, c)
        hb0 = h_gain_woven(1, 0, th0)
        g3 = gather(words3[1], list3, U32, "v3_words1", "th0")
        h_quant(1, 0, hb0)
        for c in range(MT):
            stage2_pass(e3[c], 1, g3, v3_scales, 0, c, 0, HALF)
        h_quant(1, 1, hb1)
        g2 = sb([P, S2], U32, "v2_words1", "hb11")
        th3 = []
        for c in range(MT):
            stage2_pass(e3[c], 1, g3, v3_scales, 0, c, HALF, S)
            t3 = sb([P, S], F32, f"th3_{c}")
            nc.scalar.activation(out=t3[:], in_=e3[c][:], func=ACT.Tanh)
            th3.append(t3)
        for c in range(MT):
            nc.vector.tensor_copy(out=g2[:, c * P : (c + 1) * P], in_=words2[1][:].indirect(list2[:, c * P // 16 : (c + 1) * P // 16]))
            stage2_pass(e2[c], 1, g2, v2_scales, 8, c)
        pieces = [(c, 0, S) for c in range(MT - 1)] + [(MT - 1, 0, HALF), (MT - 1, HALF, S)]
        for c, j0, j1 in pieces:
            o = sb([P, j1 - j0], F32, f"o{c}_{j0}")
            nc.vector.scalar_tensor_tensor(
                out=o[:], in0=e2[c][:, j0:j1], scalar=low_sb[:, c : c + 1], in1=th3[c][:, j0:j1], op0=ALU.max, op1=ALU.mult
            )
            nc.sync.dma_start(out=out[c * P : (c + 1) * P, j0:j1], in_=o[:])
